import numpy as np
import ml_dtypes


def mxq(x, axis, fmt="e4m3"):
    dtype, down = {"e4m3": (ml_dtypes.float8_e4m3fn, 7), "e5m2": (ml_dtypes.float8_e5m2, 14)}[fmt]
    v = np.moveaxis(np.asarray(x, np.float32).astype(ml_dtypes.bfloat16).astype(np.float64), axis, -1)
    blocks = v.reshape(v.shape[:-1] + (-1, 32))
    amax = np.abs(blocks).max(-1, keepdims=True)
    byte = np.maximum(np.where(amax > 0, np.frexp(amax)[1] - 1 + 127, 0) - down, 1)
    scale = np.exp2(byte - 127.0)
    codes = (blocks / scale).astype(np.float32).astype(dtype).astype(np.float64)
    return np.moveaxis((codes * scale).reshape(v.shape), -1, axis)


WIDE = False


def mx_kscale(k):
    if not WIDE:
        return np.ones(k)
    levels = np.array([30, -30])
    if k % 512:
        return np.exp2(np.random.permutation(np.resize(levels, k // 32))).repeat(32)
    a = np.empty((k // 512, 16))
    for p in range(k // 512):
        a[p, :8] = np.random.permutation(np.resize(levels, 8))
        for g in range(8):
            far = levels[np.abs(levels - a[p, g]) >= 10]
            a[p, g + 8] = far[np.random.randint(len(far))]
    return np.exp2(a.ravel()).repeat(32)


def f64(x):
    return np.asarray(x).astype(np.float64)


E2M1 = np.array([0.0, 0.5, 1.0, 1.5, 2.0, 3.0, 4.0, 6.0, -0.0, -0.5, -1.0, -1.5, -2.0, -3.0, -4.0, -6.0])


def pack_weight(w, fmt):
    k, n = w.shape
    w = f64(np.asarray(w, np.float32).astype(ml_dtypes.bfloat16)).reshape(k // 32, 32, n)
    amax = np.abs(w).max(1)
    if fmt == "e4m3":
        byte = np.frexp(amax)[1] - 1 + 127 - 7
    else:
        mant, ex = np.frexp(amax / 6.0)
        byte = np.where(mant > 0.5, ex, ex - 1) + 127
    byte = np.clip(np.where(amax > 0, byte, 1), 1, 254)
    scaled = (w * np.exp2(127.0 - byte)[:, None, :]).reshape(k, n).astype(np.float32)
    by_word = np.ascontiguousarray(scaled.reshape(k // 512, 128, 4, n).transpose(0, 1, 3, 2))
    if fmt == "e4m3":
        words = by_word.astype(ml_dtypes.float8_e4m3fn).view(np.uint8)
    else:
        c = by_word.astype(ml_dtypes.float4_e2m1fn).view(np.uint8) & 0xF
        words = (c[..., 0::2] | (c[..., 1::2] << 4)).reshape(k // 512, 128, 2 * n)
    return np.ascontiguousarray(words), np.ascontiguousarray(byte.astype(np.uint8).reshape(k // 512, 16, n))


def unpack_weight(words, scales, fmt):
    g, _, n = scales.shape
    words = np.ascontiguousarray(words).reshape(g, 128, n, -1)
    if fmt == "e4m3":
        vals = words.view(ml_dtypes.float8_e4m3fn).astype(np.float64)
    else:
        nib = np.empty((g, 128, n, 4), np.uint8)
        nib[..., 0::2] = words & 0xF
        nib[..., 1::2] = words >> 4
        vals = E2M1[nib]
    vals = vals * np.repeat(np.exp2(scales.astype(np.float64) - 127.0), 8, axis=1)[..., None]
    return vals.transpose(0, 1, 3, 2).reshape(g * 512, n)


O, K, M, T = 512, 1024, 512, 1536


def setup_inputs():
    n = np.random.standard_normal
    s = mx_kscale(K)[:, None]
    dy = np.exp(0.5 * n((1, T))) * n((K, T))
    w = n((K, M)) / np.sqrt(K) / s
    p_w8 = pack_weight(w[:O], "e4m3")
    p_w4 = pack_weight(w[O:], "e2m1")
    return {
        "dy": (dy * s).astype(np.float32),
        "w8_words": p_w8[0],
        "w8_scales": p_w8[1],
        "w4_words": p_w4[0],
        "w4_scales": p_w4[1],
        "r": (n((1536, 512))).astype(np.float32),
    }


def reference(dy, w8_words, w8_scales, w4_words, w4_scales, r):
    dy_ = mxq(f64(dy), 0, "e5m2")
    w8_ = unpack_weight(w8_words, w8_scales, "e4m3")
    w4_ = unpack_weight(w4_words, w4_scales, "e2m1")
    y = dy_[:O].T @ w8_ + dy_[O:].T @ w4_
    return f64(r) + y

@@ -1,0 +1,145 @@
+from contextlib import ExitStack
+
+import concourse.mybir as mybir
+
+K, T, D = 1024, 1536, 512
+FLOPS = 2 * K * T * D
+
+F32 = mybir.dt.float32
+BF16 = mybir.dt.bfloat16
+I32 = mybir.dt.int32
+U32 = mybir.dt.uint32
+U8 = mybir.dt.uint8
+E5M2 = mybir.dt.float8_e5m2_x4
+E4M3 = mybir.dt.float8_e4m3fn_x4
+E2M1 = mybir.dt.float4_e2m1fn_x4
+
+P = 128
+PACK = 4
+K_PASS = P * PACK
+PASSES = K // K_PASS
+TILES = 4
+GROUP = P * TILES
+GROUPS = T // GROUP
+BANKS = 8
+
+
+def tile_mix_dyq_tm_res_kernel(tc, dy, w8_words, w8_scales, w4_words, w4_scales, r, out):
+    nc = tc.nc
+    with ExitStack() as ctx:
+        keep = ctx.enter_context(tc.tile_pool(name="keep", bufs=1))
+        psum = ctx.enter_context(tc.psum_pool(name="psum", bufs=1))
+        ctx.enter_context(tc.manual_schedule())
+
+        raw = [keep.tile([P, PACK * T], F32, name="raw%d" % a, align_bytes=64) for a in range(PASSES)]
+        w8 = keep.tile([P, D * 4], U8, name="w8", align_bytes=64)
+        w4 = keep.tile([P, D * 2], U8, name="w4", align_bytes=64)
+        s8 = keep.tile([P, D], U8, name="s8", align_bytes=64)
+        s4 = keep.tile([P, D], U8, name="s4", align_bytes=64)
+        rt = [keep.tile([P, TILES, D], F32, name="r%d" % g, align_bytes=64) for g in range(GROUPS)]
+        ot = [keep.tile([P, TILES, D], F32, name="o%d" % g, align_bytes=64) for g in range(GROUPS)]
+        units = [(a, g) for a in range(PASSES) for g in range(GROUPS)]
+        grouped = {u: keep.tile([P, GROUP * PACK], BF16, name="grouped%d%d" % u, align_bytes=64) for u in units}
+        codes = {u: keep.tile([P, GROUP], U32, name="codes%d%d" % u, align_bytes=64) for u in units}
+        scales = {u: keep.tile([P, GROUP], U8, name="scales%d%d" % u, align_bytes=64) for u in units}
+
+        def token_rows(x, g):
+            return x[g * GROUP : (g + 1) * GROUP, :].rearrange("(m i) d -> m i d", i=TILES)
+
+        def load_dy(a):
+            nc.sync.dma_start(out=raw[a][:], in_=dy[a * K_PASS : (a + 1) * K_PASS, :].rearrange("(p j) t -> p (j t)", j=PACK))
+
+        def load_scales(queue, tile, dram):
+            for q in range(4):
+                queue.dma_start(out=tile[32 * q : 32 * q + 4, :].bitcast(I32), in_=dram[0, 4 * q : 4 * q + 4, :].bitcast(I32))
+
+        def cast(copy, a, g, m0, m1):
+            src = raw[a][:].rearrange("p (j t) -> p j t", j=PACK)[:, :, g * GROUP : (g + 1) * GROUP]
+            dst = grouped[(a, g)][:].rearrange("p (i m j) -> p m i j", i=TILES, j=PACK)
+            copy(out=dst[:, m0:m1], in_=src.rearrange("p j (m i) -> p m i j", i=TILES)[:, m0:m1])
+
+        def quantise(a, g):
+            u = (a, g)
+            nc.vector.quantize_mx(out=codes[u][:].bitcast(E5M2), scales=scales[u][:], in_=grouped[u][:])
+
+        acc = {}
+
+        def multiply(a, g, i):
+            n = g * TILES + i
+            if a == 0:
+                acc[n] = psum.tile([P, D], F32, name="acc%d" % (n % BANKS))
+            cols = slice(i * P, (i + 1) * P)
+            w, s = ((w8[:].bitcast(E4M3), s8[:]), (w4[:].bitcast(E2M1), s4[:]))[a]
+            nc.tensor.matmul_mx(
+                out=acc[n][:],
+                lhsT=codes[(a, g)][:, cols].bitcast(E5M2),
+                lhsT_scale=scales[(a, g)][:, cols],
+                rhs=w,
+                rhs_scale=s,
+                start=(a == 0),
+                stop=(a == PASSES - 1),
+            )
+
+        def add_r(g, i):
+            nc.vector.tensor_tensor(out=ot[g][:, i, :], in0=acc[g * TILES + i][:], in1=rt[g][:, i, :], op=mybir.AluOpType.add)
+
+        def store(g, i0, i1):
+            nc.sync.dma_start(out=token_rows(out, g)[:, i0:i1, :], in_=ot[g][:, i0:i1, :])
+
+        V, S = nc.vector.tensor_copy, nc.scalar.copy
+        H = P // 2
+
+        nc.vector.memset(s8[:].bitcast(I32), 0)
+        nc.vector.memset(s4[:].bitcast(I32), 0)
+        load_dy(0)
+        load_scales(nc.scalar, s8, w8_scales)
+        load_scales(nc.gpsimd, s4, w4_scales)
+        nc.sync.dma_start(out=w8[:].bitcast(I32), in_=w8_words[0].rearrange("p n t -> p (n t)").bitcast(I32))
+        load_dy(1)
+        nc.sync.dma_start(out=w4[:].bitcast(I32), in_=w4_words[0].bitcast(I32))
+        for g in range(GROUPS):
+            nc.sync.dma_start(out=rt[g][:], in_=token_rows(r, g))
+
+        cast(V, 0, 0, 0, P)
+        cast(S, 0, 1, 0, P)
+        cast(V, 0, 2, 0, H)
+        cast(S, 0, 2, H, P)
+        for g in range(GROUPS):
+            quantise(0, g)
+        for g in range(2):
+            for i in range(TILES):
+                multiply(0, g, i)
+
+        cast(V, 1, 0, 0, H)
+        cast(S, 1, 0, H, P)
+        cast(V, 1, 1, 0, 32)
+        cast(S, 1, 1, 32, P)
+        quantise(1, 0)
+        for i in range(TILES):
+            multiply(1, 0, i)
+        cast(V, 1, 2, 0, 32)
+        cast(S, 1, 2, 32, P)
+        add_r(0, 0)
+        add_r(0, 1)
+        quantise(1, 1)
+        for i in range(TILES):
+            multiply(1, 1, i)
+        add_r(0, 2)
+        add_r(0, 3)
+        store(0, 0, TILES)
+        for i in range(TILES):
+            multiply(0, 2, i)
+        add_r(1, 0)
+        add_r(1, 1)
+        quantise(1, 2)
+        for i in range(TILES):
+            multiply(1, 2, i)
+        add_r(1, 2)
+        add_r(1, 3)
+        store(1, 0, TILES)
+        add_r(2, 0)
+        add_r(2, 1)
+        store(2, 0, 2)
+        add_r(2, 2)
+        add_r(2, 3)
+        store(2, 2, TILES)

@@ -36,27 +36,34 @@ def tile_mix_dyq_tm_res_kernel(tc, dy, w8_words, w8_scales, w4_words, w4_scales,
         w4 = keep.tile([P, D * 2], U8, name="w4", align_bytes=64)
         s8 = keep.tile([P, D], U8, name="s8", align_bytes=64)
         s4 = keep.tile([P, D], U8, name="s4", align_bytes=64)
-        rt = [keep.tile([P, TILES, D], F32, name="r%d" % g, align_bytes=64) for g in range(GROUPS)]
-        ot = [keep.tile([P, TILES, D], F32, name="o%d" % g, align_bytes=64) for g in range(GROUPS)]
+        rt = [keep.tile([P, TILES * D], F32, name="r%d" % g, align_bytes=64) for g in range(GROUPS)]
+        ot = [keep.tile([P, TILES * D], F32, name="o%d" % g, align_bytes=64) for g in range(GROUPS)]
         units = [(a, g) for a in range(PASSES) for g in range(GROUPS)]
         grouped = {u: keep.tile([P, GROUP * PACK], BF16, name="grouped%d%d" % u, align_bytes=64) for u in units}
         codes = {u: keep.tile([P, GROUP], U32, name="codes%d%d" % u, align_bytes=64) for u in units}
         scales = {u: keep.tile([P, GROUP], U8, name="scales%d%d" % u, align_bytes=64) for u in units}
 
         def token_rows(x, g):
-            return x[g * GROUP : (g + 1) * GROUP, :].rearrange("(m i) d -> m i d", i=TILES)
+            return x[g * GROUP : (g + 1) * GROUP, :].rearrange("(m i) d -> m (i d)", i=TILES)
 
         def load_dy(a):
             nc.sync.dma_start(out=raw[a][:], in_=dy[a * K_PASS : (a + 1) * K_PASS, :].rearrange("(p j) t -> p (j t)", j=PACK))
+
+        def load_r(g):
+            nc.sync.dma_start(out=rt[g][:], in_=token_rows(r, g))
 
         def load_scales(queue, tile, dram):
             for q in range(4):
                 queue.dma_start(out=tile[32 * q : 32 * q + 4, :].bitcast(I32), in_=dram[0, 4 * q : 4 * q + 4, :].bitcast(I32))
 
-        def cast(copy, a, g, m0, m1):
+        def cast(copy, a, h):
+            g, i = h // 2, h % 2 * 2
             src = raw[a][:].rearrange("p (j t) -> p j t", j=PACK)[:, :, g * GROUP : (g + 1) * GROUP]
-            dst = grouped[(a, g)][:].rearrange("p (i m j) -> p m i j", i=TILES, j=PACK)
-            copy(out=dst[:, m0:m1], in_=src.rearrange("p j (m i) -> p m i j", i=TILES)[:, m0:m1])
+            dst = grouped[(a, g)][:, i * P * PACK : (i + 2) * P * PACK]
+            copy(
+                out=dst.rearrange("p (i m j) -> p m i j", i=2, j=PACK),
+                in_=src.rearrange("p j (m i) -> p m i j", i=TILES)[:, :, i : i + 2, :],
+            )
 
         def quantise(a, g):
             u = (a, g)
@@ -81,65 +88,67 @@ def tile_mix_dyq_tm_res_kernel(tc, dy, w8_words, w8_scales, w4_words, w4_scales,
             )
 
         def add_r(g, i):
-            nc.vector.tensor_tensor(out=ot[g][:, i, :], in0=acc[g * TILES + i][:], in1=rt[g][:, i, :], op=mybir.AluOpType.add)
+            cols = slice(i * D, (i + 1) * D)
+            nc.vector.tensor_tensor(out=ot[g][:, cols], in0=acc[g * TILES + i][:], in1=rt[g][:, cols], op=mybir.AluOpType.add)
 
         def store(g, i0, i1):
-            nc.sync.dma_start(out=token_rows(out, g)[:, i0:i1, :], in_=ot[g][:, i0:i1, :])
+            nc.sync.dma_start(out=token_rows(out, g)[:, i0 * D : i1 * D], in_=ot[g][:, i0 * D : i1 * D])
 
         V, S = nc.vector.tensor_copy, nc.scalar.copy
-        H = P // 2
 
         nc.vector.memset(s8[:].bitcast(I32), 0)
         nc.vector.memset(s4[:].bitcast(I32), 0)
         load_dy(0)
-        load_scales(nc.scalar, s8, w8_scales)
+        load_scales(nc.sync, s8, w8_scales)
         load_scales(nc.gpsimd, s4, w4_scales)
         nc.sync.dma_start(out=w8[:].bitcast(I32), in_=w8_words[0].rearrange("p n t -> p (n t)").bitcast(I32))
         load_dy(1)
         nc.sync.dma_start(out=w4[:].bitcast(I32), in_=w4_words[0].bitcast(I32))
         for g in range(GROUPS):
-            nc.sync.dma_start(out=rt[g][:], in_=token_rows(r, g))
+            load_r(g)
 
-        cast(V, 0, 0, 0, P)
-        cast(S, 0, 1, 0, P)
-        cast(V, 0, 2, 0, H)
-        cast(S, 0, 2, H, P)
+        for h in range(0, 2 * GROUPS, 2):
+            cast(V, 0, h)
+            cast(S, 0, h + 1)
         for g in range(GROUPS):
             quantise(0, g)
         for g in range(2):
             for i in range(TILES):
                 multiply(0, g, i)
 
-        cast(V, 1, 0, 0, H)
-        cast(S, 1, 0, H, P)
-        cast(V, 1, 1, 0, 32)
-        cast(S, 1, 1, 32, P)
+        for h in range(0, 4, 2):
+            cast(V, 1, h)
+            cast(S, 1, h + 1)
         quantise(1, 0)
         for i in range(TILES):
             multiply(1, 0, i)
-        cast(V, 1, 2, 0, 32)
-        cast(S, 1, 2, 32, P)
+        cast(V, 1, 4)
+        cast(S, 1, 5)
         add_r(0, 0)
         add_r(0, 1)
+        store(0, 0, 2)
         quantise(1, 1)
         for i in range(TILES):
             multiply(1, 1, i)
+        multiply(0, 2, 0)
+        multiply(0, 2, 1)
         add_r(0, 2)
         add_r(0, 3)
-        store(0, 0, TILES)
-        for i in range(TILES):
-            multiply(0, 2, i)
-        add_r(1, 0)
-        add_r(1, 1)
+        store(0, 2, 4)
         quantise(1, 2)
-        for i in range(TILES):
+        multiply(1, 2, 0)
+        multiply(1, 2, 1)
+        for i in range(2, TILES):
+            multiply(0, 2, i)
             multiply(1, 2, i)
-        add_r(1, 2)
-        add_r(1, 3)
-        store(1, 0, TILES)
+        for i in range(0, TILES, 2):
+            add_r(1, i)
+            add_r(1, i + 1)
+            store(1, i, i + 2)
         add_r(2, 0)
         add_r(2, 1)
         store(2, 0, 2)
         add_r(2, 2)
+        store(2, 2, 3)
         add_r(2, 3)
-        store(2, 2, TILES)
+        store(2, 3, 4)

@@ -49,8 +49,9 @@ def tile_mix_dyq_tm_res_kernel(tc, dy, w8_words, w8_scales, w4_words, w4_scales,
         def load_dy(a):
             nc.sync.dma_start(out=raw[a][:], in_=dy[a * K_PASS : (a + 1) * K_PASS, :].rearrange("(p j) t -> p (j t)", j=PACK))
 
-        def load_r(g):
-            nc.sync.dma_start(out=rt[g][:], in_=token_rows(r, g))
+        def load_r(g, i0, i1):
+            cols = slice(i0 * D, i1 * D)
+            nc.sync.dma_start(out=rt[g][:, cols], in_=token_rows(r, g)[:, cols])
 
         def load_scales(queue, tile, dram):
             for q in range(4):
@@ -65,9 +66,11 @@ def tile_mix_dyq_tm_res_kernel(tc, dy, w8_words, w8_scales, w4_words, w4_scales,
                 in_=src.rearrange("p j (m i) -> p m i j", i=TILES)[:, :, i : i + 2, :],
             )
 
-        def quantise(a, g):
-            u = (a, g)
-            nc.vector.quantize_mx(out=codes[u][:].bitcast(E5M2), scales=scales[u][:], in_=grouped[u][:])
+        def quantise(a, g, i0, i1):
+            u, cols = (a, g), slice(i0 * P, i1 * P)
+            nc.vector.quantize_mx(
+                out=codes[u][:, cols].bitcast(E5M2), scales=scales[u][:, cols], in_=grouped[u][:, i0 * P * PACK : i1 * P * PACK]
+            )
 
         acc = {}
 
@@ -91,6 +94,12 @@ def tile_mix_dyq_tm_res_kernel(tc, dy, w8_words, w8_scales, w4_words, w4_scales,
             cols = slice(i * D, (i + 1) * D)
             nc.vector.tensor_tensor(out=ot[g][:, cols], in0=acc[g * TILES + i][:], in1=rt[g][:, cols], op=mybir.AluOpType.add)
 
+        def add_r_aside(g, i):
+            cols = slice(i * D, (i + 1) * D)
+            y = keep.tile([P, D], F32, name="y%d%d" % (g, i), align_bytes=64)
+            nc.scalar.copy(out=y[:], in_=acc[g * TILES + i][:])
+            nc.gpsimd.tensor_tensor(out=ot[g][:, cols], in0=y[:], in1=rt[g][:, cols], op=mybir.AluOpType.add)
+
         def store(g, i0, i1):
             nc.sync.dma_start(out=token_rows(out, g)[:, i0 * D : i1 * D], in_=ot[g][:, i0 * D : i1 * D])
 
@@ -104,14 +113,16 @@ def tile_mix_dyq_tm_res_kernel(tc, dy, w8_words, w8_scales, w4_words, w4_scales,
         nc.sync.dma_start(out=w8[:].bitcast(I32), in_=w8_words[0].rearrange("p n t -> p (n t)").bitcast(I32))
         load_dy(1)
         nc.sync.dma_start(out=w4[:].bitcast(I32), in_=w4_words[0].bitcast(I32))
-        for g in range(GROUPS):
-            load_r(g)
+        load_r(0, 0, 2)
+        load_r(0, 2, 4)
+        load_r(1, 0, 4)
+        load_r(2, 0, 4)
 
         for h in range(0, 2 * GROUPS, 2):
             cast(V, 0, h)
             cast(S, 0, h + 1)
         for g in range(GROUPS):
-            quantise(0, g)
+            quantise(0, g, 0, TILES)
         for g in range(2):
             for i in range(TILES):
                 multiply(0, g, i)
@@ -119,32 +130,34 @@ def tile_mix_dyq_tm_res_kernel(tc, dy, w8_words, w8_scales, w4_words, w4_scales,
         for h in range(0, 4, 2):
             cast(V, 1, h)
             cast(S, 1, h + 1)
-        quantise(1, 0)
-        for i in range(TILES):
+        for i in range(0, TILES, 2):
+            quantise(1, 0, i, i + 2)
             multiply(1, 0, i)
+            multiply(1, 0, i + 1)
         cast(V, 1, 4)
         cast(S, 1, 5)
         add_r(0, 0)
         add_r(0, 1)
         store(0, 0, 2)
-        quantise(1, 1)
+        quantise(1, 1, 0, TILES)
         for i in range(TILES):
             multiply(1, 1, i)
-        multiply(0, 2, 0)
-        multiply(0, 2, 1)
+        for i in range(2):
+            multiply(0, 2, i)
         add_r(0, 2)
         add_r(0, 3)
         store(0, 2, 4)
-        quantise(1, 2)
-        multiply(1, 2, 0)
-        multiply(1, 2, 1)
+        quantise(1, 2, 0, TILES)
         for i in range(2, TILES):
             multiply(0, 2, i)
+        for i in range(TILES):
             multiply(1, 2, i)
-        for i in range(0, TILES, 2):
-            add_r(1, i)
-            add_r(1, i + 1)
-            store(1, i, i + 2)
+        add_r(1, 0)
+        add_r_aside(1, 1)
+        store(1, 0, 2)
+        add_r(1, 2)
+        add_r(1, 3)
+        store(1, 2, 4)
         add_r(2, 0)
         add_r(2, 1)
         store(2, 0, 2)

from contextlib import ExitStack

import concourse.mybir as mybir

K, T, D = 1024, 1536, 512
FLOPS = 2 * K * T * D

F32 = mybir.dt.float32
BF16 = mybir.dt.bfloat16
I32 = mybir.dt.int32
U32 = mybir.dt.uint32
U8 = mybir.dt.uint8
E5M2 = mybir.dt.float8_e5m2_x4
E4M3 = mybir.dt.float8_e4m3fn_x4
E2M1 = mybir.dt.float4_e2m1fn_x4

P = 128
PACK = 4
K_PASS = P * PACK
PASSES = K // K_PASS
TILES = 4
GROUP = P * TILES
GROUPS = T // GROUP
BANKS = 8


def tile_mix_dyq_tm_res_kernel(tc, dy, w8_words, w8_scales, w4_words, w4_scales, r, out):
    nc = tc.nc
    with ExitStack() as ctx:
        keep = ctx.enter_context(tc.tile_pool(name="keep", bufs=1))
        psum = ctx.enter_context(tc.psum_pool(name="psum", bufs=1))
        ctx.enter_context(tc.manual_schedule())

        raw = [keep.tile([P, PACK * T], F32, name="raw%d" % a, align_bytes=64) for a in range(PASSES)]
        w8 = keep.tile([P, D * 4], U8, name="w8", align_bytes=64)
        w4 = keep.tile([P, D * 2], U8, name="w4", align_bytes=64)
        s8 = keep.tile([P, D], U8, name="s8", align_bytes=64)
        s4 = keep.tile([P, D], U8, name="s4", align_bytes=64)
        rt = [keep.tile([P, TILES * D], F32, name="r%d" % g, align_bytes=64) for g in range(GROUPS)]
        ot = [keep.tile([P, TILES * D], F32, name="o%d" % g, align_bytes=64) for g in range(GROUPS)]
        units = [(a, g) for a in range(PASSES) for g in range(GROUPS)]
        grouped = {u: keep.tile([P, GROUP * PACK], BF16, name="grouped%d%d" % u, align_bytes=64) for u in units}
        codes = {u: keep.tile([P, GROUP], U32, name="codes%d%d" % u, align_bytes=64) for u in units}
        scales = {u: keep.tile([P, GROUP], U8, name="scales%d%d" % u, align_bytes=64) for u in units}

        def token_rows(x, g):
            return x[g * GROUP : (g + 1) * GROUP, :].rearrange("(m i) d -> m (i d)", i=TILES)

        def load_dy(a):
            nc.sync.dma_start(out=raw[a][:], in_=dy[a * K_PASS : (a + 1) * K_PASS, :].rearrange("(p j) t -> p (j t)", j=PACK))

        def load_r(g, i0, i1):
            cols = slice(i0 * D, i1 * D)
            nc.sync.dma_start(out=rt[g][:, cols], in_=token_rows(r, g)[:, cols])

        def load_scales(queue, tile, dram):
            for q in range(4):
                queue.dma_start(out=tile[32 * q : 32 * q + 4, :].bitcast(I32), in_=dram[0, 4 * q : 4 * q + 4, :].bitcast(I32))

        def cast(copy, a, h):
            g, i = h // 2, h % 2 * 2
            src = raw[a][:].rearrange("p (j t) -> p j t", j=PACK)[:, :, g * GROUP : (g + 1) * GROUP]
            dst = grouped[(a, g)][:, i * P * PACK : (i + 2) * P * PACK]
            copy(
                out=dst.rearrange("p (i m j) -> p m i j", i=2, j=PACK),
                in_=src.rearrange("p j (m i) -> p m i j", i=TILES)[:, :, i : i + 2, :],
            )

        def quantise(a, g, i0, i1):
            u, cols = (a, g), slice(i0 * P, i1 * P)
            nc.vector.quantize_mx(
                out=codes[u][:, cols].bitcast(E5M2), scales=scales[u][:, cols], in_=grouped[u][:, i0 * P * PACK : i1 * P * PACK]
            )

        acc = {}

        def multiply(a, g, i):
            n = g * TILES + i
            if a == 0:
                acc[n] = psum.tile([P, D], F32, name="acc%d" % (n % BANKS))
            cols = slice(i * P, (i + 1) * P)
            w, s = ((w8[:].bitcast(E4M3), s8[:]), (w4[:].bitcast(E2M1), s4[:]))[a]
            nc.tensor.matmul_mx(
                out=acc[n][:],
                lhsT=codes[(a, g)][:, cols].bitcast(E5M2),
                lhsT_scale=scales[(a, g)][:, cols],
                rhs=w,
                rhs_scale=s,
                start=(a == 0),
                stop=(a == PASSES - 1),
            )

        def add_r(g, i):
            cols = slice(i * D, (i + 1) * D)
            nc.vector.tensor_tensor(out=ot[g][:, cols], in0=acc[g * TILES + i][:], in1=rt[g][:, cols], op=mybir.AluOpType.add)

        def add_r_aside(g, i):
            cols = slice(i * D, (i + 1) * D)
            y = keep.tile([P, D], F32, name="y%d%d" % (g, i), align_bytes=64)
            nc.scalar.copy(out=y[:], in_=acc[g * TILES + i][:])
            nc.gpsimd.tensor_tensor(out=ot[g][:, cols], in0=y[:], in1=rt[g][:, cols], op=mybir.AluOpType.add)

        def store(g, i0, i1):
            nc.sync.dma_start(out=token_rows(out, g)[:, i0 * D : i1 * D], in_=ot[g][:, i0 * D : i1 * D])

        V, S = nc.vector.tensor_copy, nc.scalar.copy

        nc.vector.memset(s8[:].bitcast(I32), 0)
        nc.vector.memset(s4[:].bitcast(I32), 0)
        load_dy(0)
        load_scales(nc.sync, s8, w8_scales)
        load_scales(nc.gpsimd, s4, w4_scales)
        nc.sync.dma_start(out=w8[:].bitcast(I32), in_=w8_words[0].rearrange("p n t -> p (n t)").bitcast(I32))
        load_dy(1)
        nc.sync.dma_start(out=w4[:].bitcast(I32), in_=w4_words[0].bitcast(I32))
        load_r(0, 0, 2)
        load_r(0, 2, 4)
        load_r(1, 0, 4)
        load_r(2, 0, 4)

        for h in range(0, 2 * GROUPS, 2):
            cast(V, 0, h)
            cast(S, 0, h + 1)
        for g in range(GROUPS):
            quantise(0, g, 0, TILES)
        for g in range(2):
            for i in range(TILES):
                multiply(0, g, i)

        for h in range(0, 4, 2):
            cast(V, 1, h)
            cast(S, 1, h + 1)
        for i in range(0, TILES, 2):
            quantise(1, 0, i, i + 2)
            multiply(1, 0, i)
            multiply(1, 0, i + 1)
        cast(V, 1, 4)
        cast(S, 1, 5)
        add_r(0, 0)
        add_r(0, 1)
        store(0, 0, 2)
        quantise(1, 1, 0, TILES)
        for i in range(TILES):
            multiply(1, 1, i)
        for i in range(2):
            multiply(0, 2, i)
        add_r(0, 2)
        add_r(0, 3)
        store(0, 2, 4)
        quantise(1, 2, 0, TILES)
        for i in range(2, TILES):
            multiply(0, 2, i)
        for i in range(TILES):
            multiply(1, 2, i)
        add_r(1, 0)
        add_r_aside(1, 1)
        store(1, 0, 2)
        add_r(1, 2)
        add_r(1, 3)
        store(1, 2, 4)
        add_r(2, 0)
        add_r(2, 1)
        store(2, 0, 2)
        add_r(2, 2)
        store(2, 2, 3)
        add_r(2, 3)
        store(2, 3, 4)
